import numpy as np, ml_dtypes
CORES = [4,20,60,84,92,100,116]
N = 7
import mx_ref
NC, G = 128, 2
C = np.float32(0.01172)
BF = ml_dtypes.bfloat16
def cut(t, i, w=512):
    return t[:, w * i:w * i + w]
def tile(rs):
    return np.stack(rs, axis=2).reshape(128, -1).astype(BF)
def layer(w, X):
    out = []
    for i in range(G):
        for t in range(len(X)):
            p = mx_ref.matmul(mx_ref.quantize(cut(w, len(X) * i + t)), X[t])
            z = p if t == 0 else z + p
        out.append(z)
    return out
def act(Z):
    return [np.maximum(s * z, 0) * C for z in Z for s in (1, -1)]
def setup_inputs(rng):
    def f(*shape):
        return mx_ref.flush((rng.standard_normal(shape, dtype=np.float32) * np.exp2(rng.integers(-2, 3, shape[:-1] + (1,)))).astype(BF))
    return {"x": f(N, 128, N * 4 * NC), "w1": f(N, 128, G * 512), "w2": f(N, 128, 512)}
def setup_inputs_blocks(rng):
    d = setup_inputs(rng)
    for k in ("x", "w1", "w2"): d[k] = mx_ref.spread(d[k], rng, 4)
    return d
def setup_inputs_wide(rng):
    d = setup_inputs(rng)
    for k in ("x", "w1", "w2"): d[k] = mx_ref.flush((d[k].astype(np.float32) * np.exp2(rng.integers(-6, 7, (N, 1, 1))).astype(np.float32)).astype(BF))
    return d
def reference(x, w1, w2, own=None):
    h = np.zeros((N, 128, 4 * NC), BF)
    for c in range(N):
        for j in range(N):
            P = layer(w1[j], [mx_ref.quantize(cut(x[j], c, 4 * NC))])
            Z = P if j == 0 else [z + p for z, p in zip(Z, P)]
        h[c] = tile(act(Z))
    use = h if own is None else own["h"]
    H = [mx_ref.quantize(use[j]) for j in range(N)]
    y = np.zeros((N, 128, N * NC), np.float32)
    for r in range(N):
        qw = mx_ref.quantize(w2[r])
        for j in range(N):
            y[r][:, NC * j:NC * j + NC] = mx_ref.matmul(qw, H[j])
    return {"h": h, "y": y}

@@ -1,0 +1,361 @@
+from concourse.bass import DstId, RemoteDMATransfer
+from concourse.mybir import dt, AluOpType, ActivationFunctionType
+
+N = 7
+SIM = 128
+TW = 512
+NC = 128
+U = 256
+CACT = 0.01172
+MAXB = 2
+MAXG = 4
+
+SCRATCH = {
+    "xs": ("sbuf", [128, N * TW], "bfloat16"),
+    "w1s": ("sbuf", [128, 2 * TW], "bfloat16"),
+    "w2s": ("sbuf", [128, TW], "bfloat16"),
+    "xq": ("sbuf", [128, N * NC], "float8_e4m3fn_x4"),
+    "xp": ("sbuf", [128, N * NC], "uint8"),
+    "w1q": ("sbuf", [128, 2 * NC], "float8_e4m3fn_x4"),
+    "w1p": ("sbuf", [128, 2 * NC], "uint8"),
+    "w2q": ("sbuf", [128, NC], "float8_e4m3fn_x4"),
+    "w2p": ("sbuf", [128, NC], "uint8"),
+    "ps": ("psum", [128, 8 * 512], "float32"),
+    "part": ("sbuf", [128, (N - 1) * U], "float32"),
+    "land": ("sbuf", [128, N * U], "float32"),
+    "acc": ("sbuf", [128, U], "float32"),
+    "hs": ("sbuf", [128, TW], "bfloat16"),
+    "hq": ("sbuf", [128, N * NC], "float8_e4m3fn_x4"),
+    "hp": ("sbuf", [128, N * NC], "uint8"),
+    "ys": ("sbuf", [128, N * NC], "float32"),
+    "rl": ("sbuf", [128, MAXB * U], "float32"),
+    "rq": ("sbuf", [128, NC], "float8_e4m3fn_x4"),
+    "rp": ("sbuf", [128, NC], "uint8"),
+}
+SEMAPHORES = (["ld_w1", "ld_a", "ld_b", "ld_o", "ld_w2", "q_w1", "q_a", "q_b", "q_o", "q_w2",
+               "mm_a0", "mm_a1", "mm_b0", "mm_b1", "mm_o", "cp_a", "cp_b", "vs", "act", "hq_done",
+               "sent1", "sent2", "st", "r1", "rqc", "rqs"]
+              + ["p%d" % j for j in range(N)] + ["h%d" % j for j in range(N)]
+              + ["m2_%d" % k for k in range(N)] + ["c2_%d" % k for k in range(N)])
+
+
+def _bits(m):
+    return [e for e in range(m.bit_length()) if (m >> e) & 1]
+
+
+def _mask(es):
+    m = 0
+    for e in es:
+        m |= 1 << e
+    return m
+
+
+def _pow2(k):
+    p = 1
+    while 2 * p <= k:
+        p *= 2
+    return p
+
+
+def _deal(pool, m):
+    per = _pow2(len(pool) // m)
+    return [pool[i * per:(i + 1) * per] for i in range(m)]
+
+
+def _plan(T, topo):
+    cores = [int(c) for c in T.cores]
+    n = len(cores)
+    chips = sorted(set(topo.chip(c) for c in range(SIM)))
+
+    def route(s, d):
+        a, b, di = topo.chip(s), topo.chip(d), topo.die(s)
+        if a == b:
+            return []
+        if topo.same_plane(a, b):
+            return [("out", a, di), ("in", b, di)]
+        if topo.mates(a, b):
+            return [("mate", a, di)]
+        m = [c for c in chips if topo.mates(a, c)][0]
+        return [("mate", a, di), ("out", m, di), ("in", b, di)]
+
+    load = {}
+    direct = dict((a, []) for a in range(n))
+    for a in range(n):
+        for k in range(1, n):
+            b = (a + k) % n
+            if topo.may_write(cores[a], cores[b]):
+                direct[a].append(b)
+                for key in route(cores[a], cores[b]):
+                    load[key] = load.get(key, 0) + 1
+    helper = {}
+    for a in range(n):
+        for k in range(1, n):
+            b = (a + k) % n
+            if topo.may_write(cores[a], cores[b]):
+                continue
+            best = None
+            for r in range(SIM):
+                if topo.chip(r) != topo.chip(cores[a]) or r in cores or not topo.may_write(r, cores[b]):
+                    continue
+                have = len(helper[r][1]) if r in helper else 0
+                if have >= MAXB:
+                    continue
+                keys = route(r, cores[b]) + [("core", r)]
+                cost = (max(load.get(key, 0) + 1 for key in keys), have, topo.die(r) != topo.die(cores[a]), r)
+                if best is None or cost < best[0]:
+                    best = (cost, r, keys)
+            r = best[1]
+            helper.setdefault(r, [a, []])[1].append(b)
+            for key in best[2]:
+                load[key] = load.get(key, 0) + 1
+
+    ranks, p1cnt, eta, hinfo = {}, {}, {}, {}
+    for a in range(n):
+        me = cores[a]
+        bund = sorted([(r, sorted(v[1])) for r, v in helper.items() if v[0] == a], key=lambda t: (-len(t[1]), t[1]))
+        ga, gb = [], []
+        for r, ds in bund:
+            if sum(len(s["dests"]) for s in ga) + len(ds) <= MAXG:
+                ga.append({"to": r, "dests": ds, "relay": True})
+            else:
+                gb.append({"to": r, "dests": ds, "relay": True})
+        for b in sorted(direct[a]):
+            gb.append({"to": cores[b], "dests": [b], "relay": False})
+        slot, groups, tiles = 0, [], 2
+        for grp in (ga, gb):
+            for s in grp:
+                s["slot"] = slot
+                slot += len(s["dests"])
+            tiles += sum(len(s["dests"]) for s in grp)
+            calls = []
+            for w in sorted(set(len(s["dests"]) for s in grp), reverse=True):
+                call = [s for s in grp if len(s["dests"]) == w]
+                far = [s for s in call if topo.chip(s["to"]) != topo.chip(me)]
+                near = [s for s in call if topo.chip(s["to"]) == topo.chip(me)]
+                lo = _bits(topo.mask(me, far[0]["to"])) if far else []
+                hi = [e for e in _bits(topo.mask(me, near[0]["to"])) if e not in lo] if near else []
+                for lst, pool in ((far, lo), (near, hi)):
+                    if lst:
+                        for s, es in zip(lst, _deal(pool, len(lst))):
+                            s["eng"] = es
+                calls.append(call)
+            groups.append(calls)
+            for s in grp:
+                t = 0.5 * tiles + 12.8 * len(s["dests"]) / len(s["eng"])
+                if s["relay"]:
+                    fw = _deal(_bits(topo.mask(s["to"], cores[s["dests"][0]])), len(s["dests"]))
+                    hinfo[s["to"]] = {"src": a, "dests": s["dests"], "in1": len(s["eng"]), "fw": fw}
+                    for b, es in zip(s["dests"], fw):
+                        p1cnt[(a, b)] = len(es)
+                        eta[(a, b)] = t + 3.0 + 12.8 / len(es)
+                else:
+                    p1cnt[(a, s["dests"][0])] = len(s["eng"])
+                    eta[(a, s["dests"][0])] = t
+        hel = [s["to"] for s in ga + gb if s["relay"]]
+        lo = _bits(topo.mask(me, cores[direct[a][0]])) if direct[a] else []
+        hi = [e for e in _bits(topo.mask(me, hel[0])) if e not in lo] if hel else []
+        ranks[a] = {"groups": groups, "A": [b for s in ga for b in s["dests"]], "B": [b for s in gb for b in s["dests"]],
+                    "direct": direct[a], "helpers": hel, "lo": lo, "hi": hi}
+        for r in hel:
+            hinfo[r]["in2"] = len(hi)
+            hinfo[r]["fw2"] = _bits(topo.mask(r, cores[hinfo[r]["dests"][0]]))
+    for b in range(n):
+        src = [a for a in range(n) if a != b]
+        ranks[b]["order1"] = sorted(src, key=lambda a: (eta[(a, b)], a))
+        ranks[b]["cnt1"] = dict((a, p1cnt[(a, b)]) for a in src)
+        first = sorted([a for a in src if b in direct[a]], key=lambda a: (direct[a].index(b), a))
+        ranks[b]["order2"] = [b] + first + [a for a in src if b not in direct[a]]
+        cnt2 = {}
+        for a in src:
+            if b in direct[a]:
+                cnt2[a] = 2 * len(ranks[a]["lo"])
+            else:
+                cnt2[a] = 2 * [len(v["fw2"]) for v in hinfo.values() if v["src"] == a and b in v["dests"]][0]
+        ranks[b]["cnt2"] = cnt2
+    return {"cores": cores, "ranks": ranks, "helpers": hinfo}
+
+
+def _tr(topo, dsts, eng, sem, src, outs):
+    ids = []
+    for d in dsts:
+        a = topo.addr(d)
+        ids.append(DstId(rid=a[0], pnc=a[1]))
+    if len(dsts) == 1:
+        return RemoteDMATransfer(dst_ids=ids, dma_engine_mask=_mask(eng), remote_sem=sem, src=src, dst=outs[0])
+    return RemoteDMATransfer(dst_ids=ids, dma_engine_mask=_mask(eng), remote_sem=sem, srcs=[src], dsts=outs)
+
+
+def _helper(g, core, T, topo, P):
+    S, h, cores = T.sem, P["helpers"][core], P["cores"]
+    a, ds = h["src"], h["dests"]
+    sent = 0
+    g.wait_ge(S.r1, h["in1"])
+    g.remote_dma_fused([_tr(topo, [cores[b]], es, S["p%d" % a], T.rl[:, U * k:U * k + U], [T.land[:, U * a:U * a + U]])
+                        for k, (b, es) in enumerate(zip(ds, h["fw"]))], local_sem=S.sent1)
+    sent += sum(len(es) for es in h["fw"])
+    to = [cores[b] for b in ds]
+    g.wait_ge(S.rqc, h["in2"])
+    g.remote_dma_fused([_tr(topo, to, h["fw2"], S["h%d" % a], T.rq[:].bitcast(dt.uint8),
+                            [T.hq[:, NC * a:NC * a + NC].bitcast(dt.uint8) for b in ds])], local_sem=S.sent1)
+    g.wait_ge(S.rqs, h["in2"])
+    g.remote_dma_fused([_tr(topo, to, h["fw2"], S["h%d" % a], T.rp[:], [T.hp[:, NC * a:NC * a + NC] for b in ds])],
+                       local_sem=S.sent1)
+    sent += 2 * len(h["fw2"])
+    g.wait_ge(S.sent1, sent)
+
+
+def _rank(g, core, r, T, topo, P):
+    S, R, cores = T.sem, P["ranks"][r], P["cores"]
+    v, s, t, y = g.vector, g.scalar, g.tensor, g.sync
+    A, B = R["A"], R["B"]
+    nA, nB = len(A), len(B)
+    Copy, Relu = ActivationFunctionType.Copy, ActivationFunctionType.Relu
+
+    q = [y, s]
+    nq = [0]
+
+    def load(slots, first, sem):
+        k, m = 0, 0
+        while k < len(slots):
+            e = k + 1
+            while e < len(slots) and slots[e] == slots[e - 1] + 1:
+                e += 1
+            q[nq[0] % 2].dma_start(T.xs[:, TW * (first + k):TW * (first + e)],
+                                   T.x[:, TW * slots[k]:TW * (slots[e - 1] + 1)]).then_inc(sem, 16)
+            nq[0] += 1
+            m += 1
+            k = e
+        return 16 * m
+
+    y.dma_start(T.w1s[:], T.w1[:]).then_inc(S.ld_w1, 16)
+    nq[0] = 1
+    la = load(A, 0, S.ld_a)
+    lb = load(B, nA, S.ld_b)
+    lo = load([r], nA + nB, S.ld_o)
+    q[nq[0] % 2].dma_start(T.w2s[:], T.w2[:]).then_inc(S.ld_w2, 16)
+
+    def quant(first, cnt, ld, lcnt, sem):
+        v.wait_ge(ld, lcnt)
+        v.quantize_mx(T.xq[:, NC * first:NC * (first + cnt)], T.xp[:, NC * first:NC * (first + cnt)],
+                      T.xs[:, TW * first:TW * (first + cnt)]).then_inc(sem, 1)
+
+    def mm1(first, cnt, bank, qsem, sems):
+        t.wait_ge(qsem, 1)
+        for i in range(2):
+            t.matmul_mx(T.ps[:, 512 * (bank + i):512 * (bank + i) + NC * cnt], T.w1q[:, NC * i:NC * i + NC],
+                        T.w1p[:, NC * i:NC * i + NC], T.xq[:, NC * first:NC * (first + cnt)],
+                        T.xp[:, NC * first:NC * (first + cnt)], True, True).then_inc(sems[i], 1)
+
+    def copies(first, cnt, bank, sems, done):
+        v.wait_ge(sems[0], 1)
+        s.wait_ge(sems[1], 1)
+        for k in range(cnt):
+            o = U * (first + k)
+            v.tensor_copy(T.part[:, o:o + NC], T.ps[:, 512 * bank + NC * k:512 * bank + NC * k + NC]).then_inc(done, 1)
+            s.activation(T.part[:, o + NC:o + U], T.ps[:, 512 * (bank + 1) + NC * k:512 * (bank + 1) + NC * k + NC],
+                         Copy).then_inc(done, 1)
+
+    v.wait_ge(S.ld_w1, 16)
+    v.quantize_mx(T.w1q[:], T.w1p[:], T.w1s[:]).then_inc(S.q_w1, 1)
+    t.wait_ge(S.q_w1, 1)
+    quant(0, nA, S.ld_a, la, S.q_a)
+    mm1(0, nA, 0, S.q_a, [S.mm_a0, S.mm_a1])
+    copies(0, nA, 0, [S.mm_a0, S.mm_a1], S.cp_a)
+    quant(nA, nB, S.ld_b, lb, S.q_b)
+    mm1(nA, nB, 2, S.q_b, [S.mm_b0, S.mm_b1])
+    copies(nA, nB, 2, [S.mm_b0, S.mm_b1], S.cp_b)
+    quant(nA + nB, 1, S.ld_o, lo, S.q_o)
+    mm1(nA + nB, 1, 4, S.q_o, [S.mm_o, S.mm_o])
+    v.wait_ge(S.ld_w2, 16)
+    v.quantize_mx(T.w2q[:], T.w2p[:], T.w2s[:]).then_inc(S.q_w2, 1)
+
+    sent1 = 0
+    for calls, sem, cnt in zip(R["groups"], (S.cp_a, S.cp_b), (2 * nA, 2 * nB)):
+        g.wait_ge(sem, cnt)
+        for call in calls:
+            trs = []
+            for x in call:
+                w = len(x["dests"])
+                src = T.part[:, U * x["slot"]:U * (x["slot"] + w)]
+                if x["relay"]:
+                    trs.append(_tr(topo, [x["to"]], x["eng"], S.r1, src, [T.rl[:, 0:U * w]]))
+                else:
+                    trs.append(_tr(topo, [x["to"]], x["eng"], S["p%d" % r], src, [T.land[:, U * r:U * r + U]]))
+                sent1 += len(x["eng"])
+            g.remote_dma_fused(trs, local_sem=S.sent1)
+
+    o1, c1 = R["order1"], R["cnt1"]
+    v.wait_ge(S.mm_o, 2)
+    v.wait_ge(S["p%d" % o1[0]], c1[o1[0]])
+    for i in range(2):
+        v.tensor_tensor(T.acc[:, NC * i:NC * i + NC], T.ps[:, 512 * (4 + i):512 * (4 + i) + NC],
+                        T.land[:, U * o1[0] + NC * i:U * o1[0] + NC * i + NC], AluOpType.add).then_inc(S.vs, 1)
+    nv = 2
+    for a in o1[1:]:
+        v.wait_ge(S["p%d" % a], c1[a])
+        v.wait_ge(S.vs, nv)
+        v.tensor_tensor(T.acc[:], T.acc[:], T.land[:, U * a:U * a + U], AluOpType.add).then_inc(S.vs, 1)
+        nv += 1
+    v.wait_ge(S.vs, nv)
+    s.wait_ge(S.vs, nv)
+    for i in range(2):
+        z = T.acc[:, NC * i:NC * i + NC]
+        v.tensor_scalar(T.hs[:, 2 * i:TW:4], z, 0.0, CACT, AluOpType.max, AluOpType.mult).then_inc(S.act, 1)
+        s.activation(T.hs[:, 2 * i + 1:TW:4], z, Relu, scale=-CACT).then_inc(S.act, 1)
+    v.wait_ge(S.act, 4)
+    own = slice(NC * r, NC * r + NC)
+    v.quantize_mx(T.hq[:, own], T.hp[:, own], T.hs[:]).then_inc(S.hq_done, 1)
+
+    g.wait_ge(S.hq_done, 1)
+    sent2 = 0
+    for kind in range(2):
+        trs = []
+        if R["helpers"]:
+            trs.append(_tr(topo, R["helpers"], R["hi"], (S.rqc, S.rqs)[kind],
+                           T.hq[:, own].bitcast(dt.uint8) if kind == 0 else T.hp[:, own],
+                           [T.rq[:].bitcast(dt.uint8) if kind == 0 else T.rp[:] for x in R["helpers"]]))
+            sent2 += len(R["hi"])
+        if R["direct"]:
+            trs.append(_tr(topo, [cores[b] for b in R["direct"]], R["lo"], S["h%d" % r],
+                           T.hq[:, own].bitcast(dt.uint8) if kind == 0 else T.hp[:, own],
+                           [T.hq[:, own].bitcast(dt.uint8) if kind == 0 else T.hp[:, own] for b in R["direct"]]))
+            sent2 += len(R["lo"])
+        g.remote_dma_fused(trs, local_sem=S.sent2)
+
+    t.wait_ge(S.q_w2, 1)
+    t.wait_ge(S.cp_a, 2 * nA)
+    t.wait_ge(S.cp_b, 2 * nB)
+    t.wait_ge(S.hq_done, 1)
+    banks = [6, 7, 0, 1, 2, 3, 4]
+    stores = 0
+    for k, j in enumerate(R["order2"]):
+        if j != r:
+            t.wait_ge(S["h%d" % j], R["cnt2"][j])
+        blk = slice(NC * j, NC * j + NC)
+        pb = T.ps[:, 512 * banks[k]:512 * banks[k] + NC]
+        t.matmul_mx(pb, T.w2q[:], T.w2p[:], T.hq[:, blk], T.hp[:, blk], True, True).then_inc(S["m2_%d" % k], 1)
+        if k % 2 == 0:
+            v.wait_ge(S["m2_%d" % k], 1)
+            v.tensor_copy(T.ys[:, blk], pb).then_inc(S["c2_%d" % k], 1)
+        else:
+            s.wait_ge(S["m2_%d" % k], 1)
+            s.activation(T.ys[:, blk], pb, Copy).then_inc(S["c2_%d" % k], 1)
+        y.wait_ge(S["c2_%d" % k], 1)
+        y.dma_start(T.y[:, blk], T.ys[:, blk]).then_inc(S.st, 16)
+        stores += 16
+        if k == 0:
+            y.wait_ge(S.sent2, sent2)
+            y.dma_start(T.h[:], T.hs[:]).then_inc(S.st, 16)
+            stores += 16
+    y.wait_ge(S.st, stores)
+    g.wait_ge(S.sent1, sent1)
+    g.wait_ge(S.sent2, sent2)
+
+
+def rank_program(g, core, T, topo):
+    P = _plan(T, topo)
+    r = T.rank_of(core)
+    if r is not None:
+        _rank(g, core, r, T, topo, P)
+    elif core in P["helpers"]:
+        _helper(g, core, T, topo, P)

@@ -8,7 +8,8 @@ NC = 128
 U = 256
 CACT = 0.01172
 MAXB = 2
-MAXG = 4
+GS = 2
+NG = (N - 1 + GS - 1) // GS
 
 SCRATCH = {
     "xs": ("sbuf", [128, N * TW], "bfloat16"),
@@ -32,9 +33,10 @@ SCRATCH = {
     "rq": ("sbuf", [128, NC], "float8_e4m3fn_x4"),
     "rp": ("sbuf", [128, NC], "uint8"),
 }
-SEMAPHORES = (["ld_w1", "ld_a", "ld_b", "ld_o", "ld_w2", "q_w1", "q_a", "q_b", "q_o", "q_w2",
-               "mm_a0", "mm_a1", "mm_b0", "mm_b1", "mm_o", "cp_a", "cp_b", "vs", "act", "hq_done",
-               "sent1", "sent2", "st", "r1", "rqc", "rqs"]
+SEMAPHORES = (["ld_w1", "ld_o", "ld_w2", "q_w1", "q_o", "q_w2", "mm_o", "vs", "z0", "z1", "act", "hq_done", "go",
+               "sent1", "sent2", "st", "rqc", "rqs"]
+              + ["%s%d" % (s, i) for s in ("ld", "q", "ma", "mb", "cp") for i in range(NG)]
+              + ["r1_%d" % k for k in range(MAXB)]
               + ["p%d" % j for j in range(N)] + ["h%d" % j for j in range(N)]
               + ["m2_%d" % k for k in range(N)] + ["c2_%d" % k for k in range(N)])
 
@@ -112,53 +114,46 @@ def _plan(T, topo):
     ranks, p1cnt, eta, hinfo = {}, {}, {}, {}
     for a in range(n):
         me = cores[a]
-        bund = sorted([(r, sorted(v[1])) for r, v in helper.items() if v[0] == a], key=lambda t: (-len(t[1]), t[1]))
-        ga, gb = [], []
-        for r, ds in bund:
-            if sum(len(s["dests"]) for s in ga) + len(ds) <= MAXG:
-                ga.append({"to": r, "dests": ds, "relay": True})
-            else:
-                gb.append({"to": r, "dests": ds, "relay": True})
-        for b in sorted(direct[a]):
-            gb.append({"to": cores[b], "dests": [b], "relay": False})
-        slot, groups, tiles = 0, [], 2
-        for grp in (ga, gb):
-            for s in grp:
-                s["slot"] = slot
-                slot += len(s["dests"])
-            tiles += sum(len(s["dests"]) for s in grp)
-            calls = []
-            for w in sorted(set(len(s["dests"]) for s in grp), reverse=True):
-                call = [s for s in grp if len(s["dests"]) == w]
-                far = [s for s in call if topo.chip(s["to"]) != topo.chip(me)]
-                near = [s for s in call if topo.chip(s["to"]) == topo.chip(me)]
-                lo = _bits(topo.mask(me, far[0]["to"])) if far else []
-                hi = [e for e in _bits(topo.mask(me, near[0]["to"])) if e not in lo] if near else []
-                for lst, pool in ((far, lo), (near, hi)):
-                    if lst:
-                        for s, es in zip(lst, _deal(pool, len(lst))):
-                            s["eng"] = es
-                calls.append(call)
-            groups.append(calls)
-            for s in grp:
-                t = 0.5 * tiles + 12.8 * len(s["dests"]) / len(s["eng"])
+        hs = sorted([(r, v[1]) for r, v in helper.items() if v[0] == a], key=lambda t: (-len(t[1]), t[0]))
+        seq = []
+        for k in range(MAXB):
+            seq += [{"to": r, "dest": ds[k], "relay": True, "k": k} for r, ds in hs if len(ds) > k]
+        seq += [{"to": cores[b], "dest": b, "relay": False, "k": 0} for b in direct[a]]
+        for r, ds in hs:
+            hinfo[r] = {"src": a, "dests": ds, "in1": [0] * len(ds), "fw": _bits(topo.mask(r, cores[ds[0]]))}
+        groups = [seq[i:i + GS] for i in range(0, len(seq), GS)]
+        for gi, grp in enumerate(groups):
+            far = [s for s in grp if topo.chip(s["to"]) != topo.chip(me)]
+            near = [s for s in grp if topo.chip(s["to"]) == topo.chip(me)]
+            lo = _bits(topo.mask(me, far[0]["to"])) if far else []
+            hi = [e for e in _bits(topo.mask(me, near[0]["to"])) if e not in lo] if near else []
+            for lst, pool in ((far, lo), (near, hi)):
+                if lst:
+                    for s, es in zip(lst, _deal(pool, len(lst))):
+                        s["eng"] = es
+            for i, s in enumerate(grp):
+                s["slot"] = GS * gi + i
+                t = 0.5 * (2 + GS * (gi + 1)) + 12.8 / len(s["eng"])
                 if s["relay"]:
-                    fw = _deal(_bits(topo.mask(s["to"], cores[s["dests"][0]])), len(s["dests"]))
-                    hinfo[s["to"]] = {"src": a, "dests": s["dests"], "in1": len(s["eng"]), "fw": fw}
-                    for b, es in zip(s["dests"], fw):
-                        p1cnt[(a, b)] = len(es)
-                        eta[(a, b)] = t + 3.0 + 12.8 / len(es)
+                    hinfo[s["to"]]["in1"][s["k"]] = len(s["eng"])
+                    p1cnt[(a, s["dest"])] = len(hinfo[s["to"]]["fw"])
+                    eta[(a, s["dest"])] = t + 3.0 + 12.8 / len(hinfo[s["to"]]["fw"])
                 else:
-                    p1cnt[(a, s["dests"][0])] = len(s["eng"])
-                    eta[(a, s["dests"][0])] = t
-        hel = [s["to"] for s in ga + gb if s["relay"]]
-        lo = _bits(topo.mask(me, cores[direct[a][0]])) if direct[a] else []
-        hi = [e for e in _bits(topo.mask(me, hel[0])) if e not in lo] if hel else []
-        ranks[a] = {"groups": groups, "A": [b for s in ga for b in s["dests"]], "B": [b for s in gb for b in s["dests"]],
-                    "direct": direct[a], "helpers": hel, "lo": lo, "hi": hi}
-        for r in hel:
-            hinfo[r]["in2"] = len(hi)
-            hinfo[r]["fw2"] = _bits(topo.mask(r, cores[hinfo[r]["dests"][0]]))
+                    p1cnt[(a, s["dest"])] = len(s["eng"])
+                    eta[(a, s["dest"])] = t
+        hel = [r for r, ds in hs]
+        lo = _bits(topo.mask(me, cores[direct[a][0]]))
+        hi = [e for e in _bits(topo.mask(me, hel[0])) if e not in lo]
+        if len(hel) > 2 * len(direct[a]):
+            half = len(lo) // 2
+            tr2 = [(hel[:-1], hi, True), (hel[-1:], lo[half:], True), ([cores[b] for b in direct[a]], lo[:half], False)]
+        else:
+            tr2 = [(hel, hi, True), ([cores[b] for b in direct[a]], lo, False)]
+        for to, es, rel in tr2:
+            if rel:
+                for r in to:
+                    hinfo[r]["in2"] = len(es)
+        ranks[a] = {"groups": groups, "direct": direct[a], "tr2": tr2, "nd2": len(tr2[-1][1])}
     for b in range(n):
         src = [a for a in range(n) if a != b]
         ranks[b]["order1"] = sorted(src, key=lambda a: (eta[(a, b)], a))
@@ -168,9 +163,9 @@ def _plan(T, topo):
         cnt2 = {}
         for a in src:
             if b in direct[a]:
-                cnt2[a] = 2 * len(ranks[a]["lo"])
+                cnt2[a] = 2 * ranks[a]["nd2"]
             else:
-                cnt2[a] = 2 * [len(v["fw2"]) for v in hinfo.values() if v["src"] == a and b in v["dests"]][0]
+                cnt2[a] = 2 * [len(v["fw"]) for v in hinfo.values() if v["src"] == a and b in v["dests"]][0]
         ranks[b]["cnt2"] = cnt2
     return {"cores": cores, "ranks": ranks, "helpers": hinfo}
 
@@ -187,28 +182,29 @@ def _tr(topo, dsts, eng, sem, src, outs):
 
 def _helper(g, core, T, topo, P):
     S, h, cores = T.sem, P["helpers"][core], P["cores"]
-    a, ds = h["src"], h["dests"]
+    a, ds, fw = h["src"], h["dests"], h["fw"]
     sent = 0
-    g.wait_ge(S.r1, h["in1"])
-    g.remote_dma_fused([_tr(topo, [cores[b]], es, S["p%d" % a], T.rl[:, U * k:U * k + U], [T.land[:, U * a:U * a + U]])
-                        for k, (b, es) in enumerate(zip(ds, h["fw"]))], local_sem=S.sent1)
-    sent += sum(len(es) for es in h["fw"])
+    for k, b in enumerate(ds):
+        g.wait_ge(S["r1_%d" % k], h["in1"][k])
+        g.remote_dma_fused([_tr(topo, [cores[b]], fw, S["p%d" % a], T.rl[:, U * k:U * k + U],
+                                [T.land[:, U * a:U * a + U]])], local_sem=S.sent1)
+        sent += len(fw)
     to = [cores[b] for b in ds]
     g.wait_ge(S.rqc, h["in2"])
-    g.remote_dma_fused([_tr(topo, to, h["fw2"], S["h%d" % a], T.rq[:].bitcast(dt.uint8),
+    g.remote_dma_fused([_tr(topo, to, fw, S["h%d" % a], T.rq[:].bitcast(dt.uint8),
                             [T.hq[:, NC * a:NC * a + NC].bitcast(dt.uint8) for b in ds])], local_sem=S.sent1)
     g.wait_ge(S.rqs, h["in2"])
-    g.remote_dma_fused([_tr(topo, to, h["fw2"], S["h%d" % a], T.rp[:], [T.hp[:, NC * a:NC * a + NC] for b in ds])],
+    g.remote_dma_fused([_tr(topo, to, fw, S["h%d" % a], T.rp[:], [T.hp[:, NC * a:NC * a + NC] for b in ds])],
                        local_sem=S.sent1)
-    sent += 2 * len(h["fw2"])
+    sent += 2 * len(fw)
     g.wait_ge(S.sent1, sent)
 
 
 def _rank(g, core, r, T, topo, P):
     S, R, cores = T.sem, P["ranks"][r], P["cores"]
     v, s, t, y = g.vector, g.scalar, g.tensor, g.sync
-    A, B = R["A"], R["B"]
-    nA, nB = len(A), len(B)
+    G = R["groups"]
+    nsl = sum(len(grp) for grp in G)
     Copy, Relu = ActivationFunctionType.Copy, ActivationFunctionType.Relu
 
     q = [y, s]
@@ -229,10 +225,10 @@ def _rank(g, core, r, T, topo, P):
 
     y.dma_start(T.w1s[:], T.w1[:]).then_inc(S.ld_w1, 16)
     nq[0] = 1
-    la = load(A, 0, S.ld_a)
-    lb = load(B, nA, S.ld_b)
-    lo = load([r], nA + nB, S.ld_o)
-    q[nq[0] % 2].dma_start(T.w2s[:], T.w2[:]).then_inc(S.ld_w2, 16)
+    lc = [load([x["dest"] for x in grp], grp[0]["slot"], S["ld%d" % i]) for i, grp in enumerate(G)]
+    lo = load([r], nsl, S.ld_o)
+    y.wait_ge(S.go, 1)
+    y.dma_start(T.w2s[:], T.w2[:]).then_inc(S.ld_w2, 16)
 
     def quant(first, cnt, ld, lcnt, sem):
         v.wait_ge(ld, lcnt)
@@ -258,81 +254,85 @@ def _rank(g, core, r, T, topo, P):
     v.wait_ge(S.ld_w1, 16)
     v.quantize_mx(T.w1q[:], T.w1p[:], T.w1s[:]).then_inc(S.q_w1, 1)
     t.wait_ge(S.q_w1, 1)
-    quant(0, nA, S.ld_a, la, S.q_a)
-    mm1(0, nA, 0, S.q_a, [S.mm_a0, S.mm_a1])
-    copies(0, nA, 0, [S.mm_a0, S.mm_a1], S.cp_a)
-    quant(nA, nB, S.ld_b, lb, S.q_b)
-    mm1(nA, nB, 2, S.q_b, [S.mm_b0, S.mm_b1])
-    copies(nA, nB, 2, [S.mm_b0, S.mm_b1], S.cp_b)
-    quant(nA + nB, 1, S.ld_o, lo, S.q_o)
-    mm1(nA + nB, 1, 4, S.q_o, [S.mm_o, S.mm_o])
-    v.wait_ge(S.ld_w2, 16)
-    v.quantize_mx(T.w2q[:], T.w2p[:], T.w2s[:]).then_inc(S.q_w2, 1)
+    for i, grp in enumerate(G):
+        f, c = grp[0]["slot"], len(grp)
+        quant(f, c, S["ld%d" % i], lc[i], S["q%d" % i])
+        mm1(f, c, 2 * i, S["q%d" % i], [S["ma%d" % i], S["mb%d" % i]])
+        copies(f, c, 2 * i, [S["ma%d" % i], S["mb%d" % i]], S["cp%d" % i])
+    ob = 2 * len(G)
+    quant(nsl, 1, S.ld_o, lo, S.q_o)
+    mm1(nsl, 1, ob, S.q_o, [S.mm_o, S.mm_o])
 
     sent1 = 0
-    for calls, sem, cnt in zip(R["groups"], (S.cp_a, S.cp_b), (2 * nA, 2 * nB)):
-        g.wait_ge(sem, cnt)
-        for call in calls:
-            trs = []
-            for x in call:
-                w = len(x["dests"])
-                src = T.part[:, U * x["slot"]:U * (x["slot"] + w)]
-                if x["relay"]:
-                    trs.append(_tr(topo, [x["to"]], x["eng"], S.r1, src, [T.rl[:, 0:U * w]]))
-                else:
-                    trs.append(_tr(topo, [x["to"]], x["eng"], S["p%d" % r], src, [T.land[:, U * r:U * r + U]]))
-                sent1 += len(x["eng"])
-            g.remote_dma_fused(trs, local_sem=S.sent1)
+    for i, grp in enumerate(G):
+        g.wait_ge(S["cp%d" % i], 2 * len(grp))
+        trs = []
+        for x in grp:
+            src = T.part[:, U * x["slot"]:U * x["slot"] + U]
+            if x["relay"]:
+                trs.append(_tr(topo, [x["to"]], x["eng"], S["r1_%d" % x["k"]], src, [T.rl[:, U * x["k"]:U * x["k"] + U]]))
+            else:
+                trs.append(_tr(topo, [x["to"]], x["eng"], S["p%d" % r], src, [T.land[:, U * r:U * r + U]]))
+            sent1 += len(x["eng"])
+        g.remote_dma_fused(trs, local_sem=S.sent1)
+    g.sem_inc(S.go, 1)
 
     o1, c1 = R["order1"], R["cnt1"]
     v.wait_ge(S.mm_o, 2)
     v.wait_ge(S["p%d" % o1[0]], c1[o1[0]])
     for i in range(2):
-        v.tensor_tensor(T.acc[:, NC * i:NC * i + NC], T.ps[:, 512 * (4 + i):512 * (4 + i) + NC],
+        v.tensor_tensor(T.acc[:, NC * i:NC * i + NC], T.ps[:, 512 * (ob + i):512 * (ob + i) + NC],
                         T.land[:, U * o1[0] + NC * i:U * o1[0] + NC * i + NC], AluOpType.add).then_inc(S.vs, 1)
     nv = 2
-    for a in o1[1:]:
+    for a in o1[1:-1]:
         v.wait_ge(S["p%d" % a], c1[a])
         v.wait_ge(S.vs, nv)
         v.tensor_tensor(T.acc[:], T.acc[:], T.land[:, U * a:U * a + U], AluOpType.add).then_inc(S.vs, 1)
         nv += 1
+    a = o1[-1]
+    v.wait_ge(S["p%d" % a], c1[a])
     v.wait_ge(S.vs, nv)
-    s.wait_ge(S.vs, nv)
-    for i in range(2):
-        z = T.acc[:, NC * i:NC * i + NC]
-        v.tensor_scalar(T.hs[:, 2 * i:TW:4], z, 0.0, CACT, AluOpType.max, AluOpType.mult).then_inc(S.act, 1)
-        s.activation(T.hs[:, 2 * i + 1:TW:4], z, Relu, scale=-CACT).then_inc(S.act, 1)
+    z = [T.acc[:, 0:NC], T.acc[:, NC:U]]
+    v.tensor_tensor(z[0], z[0], T.land[:, U * a:U * a + NC], AluOpType.add).then_inc(S.z0, 1)
+    v.tensor_tensor(z[1], z[1], T.land[:, U * a + NC:U * a + U], AluOpType.add).then_inc(S.z1, 1)
+    s.wait_ge(S.z0, 1)
+    s.activation(T.hs[:, 0:TW:4], z[0], Relu, scale=CACT).then_inc(S.act, 1)
+    s.activation(T.hs[:, 1:TW:4], z[0], Relu, scale=-CACT).then_inc(S.act, 1)
+    v.wait_ge(S.z1, 1)
+    s.wait_ge(S.z1, 1)
+    v.tensor_scalar(T.hs[:, 2:TW:4], z[1], 0.0, CACT, AluOpType.max, AluOpType.mult).then_inc(S.act, 1)
+    s.activation(T.hs[:, 3:TW:4], z[1], Relu, scale=-CACT).then_inc(S.act, 1)
     v.wait_ge(S.act, 4)
     own = slice(NC * r, NC * r + NC)
     v.quantize_mx(T.hq[:, own], T.hp[:, own], T.hs[:]).then_inc(S.hq_done, 1)
+    v.wait_ge(S.ld_w2, 16)
+    v.quantize_mx(T.w2q[:], T.w2p[:], T.w2s[:]).then_inc(S.q_w2, 1)
 
     g.wait_ge(S.hq_done, 1)
     sent2 = 0
     for kind in range(2):
         trs = []
-        if R["helpers"]:
-            trs.append(_tr(topo, R["helpers"], R["hi"], (S.rqc, S.rqs)[kind],
-                           T.hq[:, own].bitcast(dt.uint8) if kind == 0 else T.hp[:, own],
-                           [T.rq[:].bitcast(dt.uint8) if kind == 0 else T.rp[:] for x in R["helpers"]]))
-            sent2 += len(R["hi"])
-        if R["direct"]:
-            trs.append(_tr(topo, [cores[b] for b in R["direct"]], R["lo"], S["h%d" % r],
-                           T.hq[:, own].bitcast(dt.uint8) if kind == 0 else T.hp[:, own],
-                           [T.hq[:, own].bitcast(dt.uint8) if kind == 0 else T.hp[:, own] for b in R["direct"]]))
-            sent2 += len(R["lo"])
+        src = T.hq[:, own].bitcast(dt.uint8) if kind == 0 else T.hp[:, own]
+        for to, es, rel in R["tr2"]:
+            if rel:
+                trs.append(_tr(topo, to, es, (S.rqc, S.rqs)[kind], src,
+                               [T.rq[:].bitcast(dt.uint8) if kind == 0 else T.rp[:] for x in to]))
+            else:
+                trs.append(_tr(topo, to, es, S["h%d" % r], src,
+                               [T.hq[:, own].bitcast(dt.uint8) if kind == 0 else T.hp[:, own] for x in to]))
+            sent2 += len(es)
         g.remote_dma_fused(trs, local_sem=S.sent2)
 
     t.wait_ge(S.q_w2, 1)
-    t.wait_ge(S.cp_a, 2 * nA)
-    t.wait_ge(S.cp_b, 2 * nB)
+    for i, grp in enumerate(G):
+        t.wait_ge(S["cp%d" % i], 2 * len(grp))
     t.wait_ge(S.hq_done, 1)
-    banks = [6, 7, 0, 1, 2, 3, 4]
     stores = 0
     for k, j in enumerate(R["order2"]):
         if j != r:
             t.wait_ge(S["h%d" % j], R["cnt2"][j])
         blk = slice(NC * j, NC * j + NC)
-        pb = T.ps[:, 512 * banks[k]:512 * banks[k] + NC]
+        pb = T.ps[:, 512 * k:512 * k + NC]
         t.matmul_mx(pb, T.w2q[:], T.w2p[:], T.hq[:, blk], T.hp[:, blk], True, True).then_inc(S["m2_%d" % k], 1)
         if k % 2 == 0:
             v.wait_ge(S["m2_%d" % k], 1)

from concourse.bass import DstId, RemoteDMATransfer
from concourse.mybir import dt, AluOpType, ActivationFunctionType

N = 7
SIM = 128
TW = 512
NC = 128
U = 256
CACT = 0.01172
MAXB = 2
GS = 2
NG = (N - 1 + GS - 1) // GS

SCRATCH = {
    "xs": ("sbuf", [128, N * TW], "bfloat16"),
    "w1s": ("sbuf", [128, 2 * TW], "bfloat16"),
    "w2s": ("sbuf", [128, TW], "bfloat16"),
    "xq": ("sbuf", [128, N * NC], "float8_e4m3fn_x4"),
    "xp": ("sbuf", [128, N * NC], "uint8"),
    "w1q": ("sbuf", [128, 2 * NC], "float8_e4m3fn_x4"),
    "w1p": ("sbuf", [128, 2 * NC], "uint8"),
    "w2q": ("sbuf", [128, NC], "float8_e4m3fn_x4"),
    "w2p": ("sbuf", [128, NC], "uint8"),
    "ps": ("psum", [128, 8 * 512], "float32"),
    "part": ("sbuf", [128, (N - 1) * U], "float32"),
    "land": ("sbuf", [128, N * U], "float32"),
    "acc": ("sbuf", [128, U], "float32"),
    "hs": ("sbuf", [128, TW], "bfloat16"),
    "hq": ("sbuf", [128, N * NC], "float8_e4m3fn_x4"),
    "hp": ("sbuf", [128, N * NC], "uint8"),
    "ys": ("sbuf", [128, N * NC], "float32"),
    "rl": ("sbuf", [128, MAXB * U], "float32"),
    "rq": ("sbuf", [128, NC], "float8_e4m3fn_x4"),
    "rp": ("sbuf", [128, NC], "uint8"),
}
SEMAPHORES = (["ld_w1", "ld_o", "ld_w2", "q_w1", "q_o", "q_w2", "mm_o", "vs", "z0", "z1", "act", "hq_done", "go",
               "sent1", "sent2", "st", "rqc", "rqs"]
              + ["%s%d" % (s, i) for s in ("ld", "q", "ma", "mb", "cp") for i in range(NG)]
              + ["r1_%d" % k for k in range(MAXB)]
              + ["p%d" % j for j in range(N)] + ["h%d" % j for j in range(N)]
              + ["m2_%d" % k for k in range(N)] + ["c2_%d" % k for k in range(N)])


def _bits(m):
    return [e for e in range(m.bit_length()) if (m >> e) & 1]


def _mask(es):
    m = 0
    for e in es:
        m |= 1 << e
    return m


def _pow2(k):
    p = 1
    while 2 * p <= k:
        p *= 2
    return p


def _deal(pool, m):
    per = _pow2(len(pool) // m)
    return [pool[i * per:(i + 1) * per] for i in range(m)]


def _plan(T, topo):
    cores = [int(c) for c in T.cores]
    n = len(cores)
    chips = sorted(set(topo.chip(c) for c in range(SIM)))

    def route(s, d):
        a, b, di = topo.chip(s), topo.chip(d), topo.die(s)
        if a == b:
            return []
        if topo.same_plane(a, b):
            return [("out", a, di), ("in", b, di)]
        if topo.mates(a, b):
            return [("mate", a, di)]
        m = [c for c in chips if topo.mates(a, c)][0]
        return [("mate", a, di), ("out", m, di), ("in", b, di)]

    load = {}
    direct = dict((a, []) for a in range(n))
    for a in range(n):
        for k in range(1, n):
            b = (a + k) % n
            if topo.may_write(cores[a], cores[b]):
                direct[a].append(b)
                for key in route(cores[a], cores[b]):
                    load[key] = load.get(key, 0) + 1
    helper = {}
    for a in range(n):
        for k in range(1, n):
            b = (a + k) % n
            if topo.may_write(cores[a], cores[b]):
                continue
            best = None
            for r in range(SIM):
                if topo.chip(r) != topo.chip(cores[a]) or r in cores or not topo.may_write(r, cores[b]):
                    continue
                have = len(helper[r][1]) if r in helper else 0
                if have >= MAXB:
                    continue
                keys = route(r, cores[b]) + [("core", r)]
                cost = (max(load.get(key, 0) + 1 for key in keys), have, topo.die(r) != topo.die(cores[a]), r)
                if best is None or cost < best[0]:
                    best = (cost, r, keys)
            r = best[1]
            helper.setdefault(r, [a, []])[1].append(b)
            for key in best[2]:
                load[key] = load.get(key, 0) + 1

    ranks, p1cnt, eta, hinfo = {}, {}, {}, {}
    for a in range(n):
        me = cores[a]
        hs = sorted([(r, v[1]) for r, v in helper.items() if v[0] == a], key=lambda t: (-len(t[1]), t[0]))
        seq = []
        for k in range(MAXB):
            seq += [{"to": r, "dest": ds[k], "relay": True, "k": k} for r, ds in hs if len(ds) > k]
        seq += [{"to": cores[b], "dest": b, "relay": False, "k": 0} for b in direct[a]]
        for r, ds in hs:
            hinfo[r] = {"src": a, "dests": ds, "in1": [0] * len(ds), "fw": _bits(topo.mask(r, cores[ds[0]]))}
        groups = [seq[i:i + GS] for i in range(0, len(seq), GS)]
        for gi, grp in enumerate(groups):
            far = [s for s in grp if topo.chip(s["to"]) != topo.chip(me)]
            near = [s for s in grp if topo.chip(s["to"]) == topo.chip(me)]
            lo = _bits(topo.mask(me, far[0]["to"])) if far else []
            hi = [e for e in _bits(topo.mask(me, near[0]["to"])) if e not in lo] if near else []
            for lst, pool in ((far, lo), (near, hi)):
                if lst:
                    for s, es in zip(lst, _deal(pool, len(lst))):
                        s["eng"] = es
            for i, s in enumerate(grp):
                s["slot"] = GS * gi + i
                t = 0.5 * (2 + GS * (gi + 1)) + 12.8 / len(s["eng"])
                if s["relay"]:
                    hinfo[s["to"]]["in1"][s["k"]] = len(s["eng"])
                    p1cnt[(a, s["dest"])] = len(hinfo[s["to"]]["fw"])
                    eta[(a, s["dest"])] = t + 3.0 + 12.8 / len(hinfo[s["to"]]["fw"])
                else:
                    p1cnt[(a, s["dest"])] = len(s["eng"])
                    eta[(a, s["dest"])] = t
        hel = [r for r, ds in hs]
        lo = _bits(topo.mask(me, cores[direct[a][0]]))
        hi = [e for e in _bits(topo.mask(me, hel[0])) if e not in lo]
        if len(hel) > 2 * len(direct[a]):
            half = len(lo) // 2
            tr2 = [(hel[:-1], hi, True), (hel[-1:], lo[half:], True), ([cores[b] for b in direct[a]], lo[:half], False)]
        else:
            tr2 = [(hel, hi, True), ([cores[b] for b in direct[a]], lo, False)]
        for to, es, rel in tr2:
            if rel:
                for r in to:
                    hinfo[r]["in2"] = len(es)
        ranks[a] = {"groups": groups, "direct": direct[a], "tr2": tr2, "nd2": len(tr2[-1][1])}
    for b in range(n):
        src = [a for a in range(n) if a != b]
        ranks[b]["order1"] = sorted(src, key=lambda a: (eta[(a, b)], a))
        ranks[b]["cnt1"] = dict((a, p1cnt[(a, b)]) for a in src)
        first = sorted([a for a in src if b in direct[a]], key=lambda a: (direct[a].index(b), a))
        ranks[b]["order2"] = [b] + first + [a for a in src if b not in direct[a]]
        cnt2 = {}
        for a in src:
            if b in direct[a]:
                cnt2[a] = 2 * ranks[a]["nd2"]
            else:
                cnt2[a] = 2 * [len(v["fw"]) for v in hinfo.values() if v["src"] == a and b in v["dests"]][0]
        ranks[b]["cnt2"] = cnt2
    return {"cores": cores, "ranks": ranks, "helpers": hinfo}


def _tr(topo, dsts, eng, sem, src, outs):
    ids = []
    for d in dsts:
        a = topo.addr(d)
        ids.append(DstId(rid=a[0], pnc=a[1]))
    if len(dsts) == 1:
        return RemoteDMATransfer(dst_ids=ids, dma_engine_mask=_mask(eng), remote_sem=sem, src=src, dst=outs[0])
    return RemoteDMATransfer(dst_ids=ids, dma_engine_mask=_mask(eng), remote_sem=sem, srcs=[src], dsts=outs)


def _helper(g, core, T, topo, P):
    S, h, cores = T.sem, P["helpers"][core], P["cores"]
    a, ds, fw = h["src"], h["dests"], h["fw"]
    sent = 0
    for k, b in enumerate(ds):
        g.wait_ge(S["r1_%d" % k], h["in1"][k])
        g.remote_dma_fused([_tr(topo, [cores[b]], fw, S["p%d" % a], T.rl[:, U * k:U * k + U],
                                [T.land[:, U * a:U * a + U]])], local_sem=S.sent1)
        sent += len(fw)
    to = [cores[b] for b in ds]
    g.wait_ge(S.rqc, h["in2"])
    g.remote_dma_fused([_tr(topo, to, fw, S["h%d" % a], T.rq[:].bitcast(dt.uint8),
                            [T.hq[:, NC * a:NC * a + NC].bitcast(dt.uint8) for b in ds])], local_sem=S.sent1)
    g.wait_ge(S.rqs, h["in2"])
    g.remote_dma_fused([_tr(topo, to, fw, S["h%d" % a], T.rp[:], [T.hp[:, NC * a:NC * a + NC] for b in ds])],
                       local_sem=S.sent1)
    sent += 2 * len(fw)
    g.wait_ge(S.sent1, sent)


def _rank(g, core, r, T, topo, P):
    S, R, cores = T.sem, P["ranks"][r], P["cores"]
    v, s, t, y = g.vector, g.scalar, g.tensor, g.sync
    G = R["groups"]
    nsl = sum(len(grp) for grp in G)
    Copy, Relu = ActivationFunctionType.Copy, ActivationFunctionType.Relu

    q = [y, s]
    nq = [0]

    def load(slots, first, sem):
        k, m = 0, 0
        while k < len(slots):
            e = k + 1
            while e < len(slots) and slots[e] == slots[e - 1] + 1:
                e += 1
            q[nq[0] % 2].dma_start(T.xs[:, TW * (first + k):TW * (first + e)],
                                   T.x[:, TW * slots[k]:TW * (slots[e - 1] + 1)]).then_inc(sem, 16)
            nq[0] += 1
            m += 1
            k = e
        return 16 * m

    y.dma_start(T.w1s[:], T.w1[:]).then_inc(S.ld_w1, 16)
    nq[0] = 1
    lc = [load([x["dest"] for x in grp], grp[0]["slot"], S["ld%d" % i]) for i, grp in enumerate(G)]
    lo = load([r], nsl, S.ld_o)
    y.wait_ge(S.go, 1)
    y.dma_start(T.w2s[:], T.w2[:]).then_inc(S.ld_w2, 16)

    def quant(first, cnt, ld, lcnt, sem):
        v.wait_ge(ld, lcnt)
        v.quantize_mx(T.xq[:, NC * first:NC * (first + cnt)], T.xp[:, NC * first:NC * (first + cnt)],
                      T.xs[:, TW * first:TW * (first + cnt)]).then_inc(sem, 1)

    def mm1(first, cnt, bank, qsem, sems):
        t.wait_ge(qsem, 1)
        for i in range(2):
            t.matmul_mx(T.ps[:, 512 * (bank + i):512 * (bank + i) + NC * cnt], T.w1q[:, NC * i:NC * i + NC],
                        T.w1p[:, NC * i:NC * i + NC], T.xq[:, NC * first:NC * (first + cnt)],
                        T.xp[:, NC * first:NC * (first + cnt)], True, True).then_inc(sems[i], 1)

    def copies(first, cnt, bank, sems, done):
        v.wait_ge(sems[0], 1)
        s.wait_ge(sems[1], 1)
        for k in range(cnt):
            o = U * (first + k)
            v.tensor_copy(T.part[:, o:o + NC], T.ps[:, 512 * bank + NC * k:512 * bank + NC * k + NC]).then_inc(done, 1)
            s.activation(T.part[:, o + NC:o + U], T.ps[:, 512 * (bank + 1) + NC * k:512 * (bank + 1) + NC * k + NC],
                         Copy).then_inc(done, 1)

    v.wait_ge(S.ld_w1, 16)
    v.quantize_mx(T.w1q[:], T.w1p[:], T.w1s[:]).then_inc(S.q_w1, 1)
    t.wait_ge(S.q_w1, 1)
    for i, grp in enumerate(G):
        f, c = grp[0]["slot"], len(grp)
        quant(f, c, S["ld%d" % i], lc[i], S["q%d" % i])
        mm1(f, c, 2 * i, S["q%d" % i], [S["ma%d" % i], S["mb%d" % i]])
        copies(f, c, 2 * i, [S["ma%d" % i], S["mb%d" % i]], S["cp%d" % i])
    ob = 2 * len(G)
    quant(nsl, 1, S.ld_o, lo, S.q_o)
    mm1(nsl, 1, ob, S.q_o, [S.mm_o, S.mm_o])

    sent1 = 0
    for i, grp in enumerate(G):
        g.wait_ge(S["cp%d" % i], 2 * len(grp))
        trs = []
        for x in grp:
            src = T.part[:, U * x["slot"]:U * x["slot"] + U]
            if x["relay"]:
                trs.append(_tr(topo, [x["to"]], x["eng"], S["r1_%d" % x["k"]], src, [T.rl[:, U * x["k"]:U * x["k"] + U]]))
            else:
                trs.append(_tr(topo, [x["to"]], x["eng"], S["p%d" % r], src, [T.land[:, U * r:U * r + U]]))
            sent1 += len(x["eng"])
        g.remote_dma_fused(trs, local_sem=S.sent1)
    g.sem_inc(S.go, 1)

    o1, c1 = R["order1"], R["cnt1"]
    v.wait_ge(S.mm_o, 2)
    v.wait_ge(S["p%d" % o1[0]], c1[o1[0]])
    for i in range(2):
        v.tensor_tensor(T.acc[:, NC * i:NC * i + NC], T.ps[:, 512 * (ob + i):512 * (ob + i) + NC],
                        T.land[:, U * o1[0] + NC * i:U * o1[0] + NC * i + NC], AluOpType.add).then_inc(S.vs, 1)
    nv = 2
    for a in o1[1:-1]:
        v.wait_ge(S["p%d" % a], c1[a])
        v.wait_ge(S.vs, nv)
        v.tensor_tensor(T.acc[:], T.acc[:], T.land[:, U * a:U * a + U], AluOpType.add).then_inc(S.vs, 1)
        nv += 1
    a = o1[-1]
    v.wait_ge(S["p%d" % a], c1[a])
    v.wait_ge(S.vs, nv)
    z = [T.acc[:, 0:NC], T.acc[:, NC:U]]
    v.tensor_tensor(z[0], z[0], T.land[:, U * a:U * a + NC], AluOpType.add).then_inc(S.z0, 1)
    v.tensor_tensor(z[1], z[1], T.land[:, U * a + NC:U * a + U], AluOpType.add).then_inc(S.z1, 1)
    s.wait_ge(S.z0, 1)
    s.activation(T.hs[:, 0:TW:4], z[0], Relu, scale=CACT).then_inc(S.act, 1)
    s.activation(T.hs[:, 1:TW:4], z[0], Relu, scale=-CACT).then_inc(S.act, 1)
    v.wait_ge(S.z1, 1)
    s.wait_ge(S.z1, 1)
    v.tensor_scalar(T.hs[:, 2:TW:4], z[1], 0.0, CACT, AluOpType.max, AluOpType.mult).then_inc(S.act, 1)
    s.activation(T.hs[:, 3:TW:4], z[1], Relu, scale=-CACT).then_inc(S.act, 1)
    v.wait_ge(S.act, 4)
    own = slice(NC * r, NC * r + NC)
    v.quantize_mx(T.hq[:, own], T.hp[:, own], T.hs[:]).then_inc(S.hq_done, 1)
    v.wait_ge(S.ld_w2, 16)
    v.quantize_mx(T.w2q[:], T.w2p[:], T.w2s[:]).then_inc(S.q_w2, 1)

    g.wait_ge(S.hq_done, 1)
    sent2 = 0
    for kind in range(2):
        trs = []
        src = T.hq[:, own].bitcast(dt.uint8) if kind == 0 else T.hp[:, own]
        for to, es, rel in R["tr2"]:
            if rel:
                trs.append(_tr(topo, to, es, (S.rqc, S.rqs)[kind], src,
                               [T.rq[:].bitcast(dt.uint8) if kind == 0 else T.rp[:] for x in to]))
            else:
                trs.append(_tr(topo, to, es, S["h%d" % r], src,
                               [T.hq[:, own].bitcast(dt.uint8) if kind == 0 else T.hp[:, own] for x in to]))
            sent2 += len(es)
        g.remote_dma_fused(trs, local_sem=S.sent2)

    t.wait_ge(S.q_w2, 1)
    for i, grp in enumerate(G):
        t.wait_ge(S["cp%d" % i], 2 * len(grp))
    t.wait_ge(S.hq_done, 1)
    stores = 0
    for k, j in enumerate(R["order2"]):
        if j != r:
            t.wait_ge(S["h%d" % j], R["cnt2"][j])
        blk = slice(NC * j, NC * j + NC)
        pb = T.ps[:, 512 * k:512 * k + NC]
        t.matmul_mx(pb, T.w2q[:], T.w2p[:], T.hq[:, blk], T.hp[:, blk], True, True).then_inc(S["m2_%d" % k], 1)
        if k % 2 == 0:
            v.wait_ge(S["m2_%d" % k], 1)
            v.tensor_copy(T.ys[:, blk], pb).then_inc(S["c2_%d" % k], 1)
        else:
            s.wait_ge(S["m2_%d" % k], 1)
            s.activation(T.ys[:, blk], pb, Copy).then_inc(S["c2_%d" % k], 1)
        y.wait_ge(S["c2_%d" % k], 1)
        y.dma_start(T.y[:, blk], T.ys[:, blk]).then_inc(S.st, 16)
        stores += 16
        if k == 0:
            y.wait_ge(S.sent2, sent2)
            y.dma_start(T.h[:], T.hs[:]).then_inc(S.st, 16)
            stores += 16
    y.wait_ge(S.st, stores)
    g.wait_ge(S.sent1, sent1)
    g.wait_ge(S.sent2, sent2)


def rank_program(g, core, T, topo):
    P = _plan(T, topo)
    r = T.rank_of(core)
    if r is not None:
        _rank(g, core, r, T, topo, P)
    elif core in P["helpers"]:
        _helper(g, core, T, topo, P)
